import numpy as np, ml_dtypes
CORES = [23,119,17,113]
N = 4
BF = ml_dtypes.bfloat16
def gentries(a):
    return np.ascontiguousarray(a.reshape(8, 16, -1).transpose(0, 2, 1)).reshape(8, -1)
def gtable(e):
    e = np.asarray(e); return np.ascontiguousarray(e.reshape(8, -1, 16).transpose(0, 2, 1)).reshape(128, -1).astype(np.int32)
G, C, P, RO, YC = 256, 16, 32, 2, 16
W, LG, LC, H, M = 4096, 8, 4, 128, 64
BIG = 2 ** 24
def probes(u, k):
    return (((u * u) >> 5)[..., None] + u[..., None] * k) & (W - 1)
def base(rng):
    ring = rng.integers(0, 256, (8, 8, 64, 16)); a = rng.integers(0, 8, (N, 8, G, 1)); b = rng.integers(0, 64, (N, 8, G, 1))
    X = ring[np.arange(8)[None, :, None, None], a, (b + np.arange(C)) & 63]
    X = np.clip(X + rng.integers(-4, 5, X.shape), 0, 255)
    th = np.where(rng.random((N, 8, P)) < 0.25, rng.integers(0, 300, (N, 8, P)), rng.integers(600, 1600, (N, 8, P)))
    return X, rng.integers(1, 256, (N, 8, 16)), rng.integers(0, 2048, (N, 8, RO, P)), th
def pack(X, wt, km, th):
    X = np.ascontiguousarray(X.reshape(N, 8, G, C, 16).transpose(0, 1, 4, 2, 3)).reshape(N, 128, W)
    return {"gen0": X.astype(np.float32).astype(BF), "wt": np.ascontiguousarray(wt.reshape(N, 128, 1)).astype(np.int32),
            "km": np.stack([gtable(a.reshape(8, -1)) for a in km]), "th": np.stack([gtable(a) for a in th])}
def setup_inputs(rng):
    return pack(*base(rng))
def column(rng, w, u):
    x = rng.integers(0, 256, 16); r = (int(u) - int(np.sum(w[2:] * x[2:]))) & (W - 1); x[0] = r & 15; x[1] = r >> 4
    return x
def link(rng, Y, w, k, o, alone=False):
    c = probes(np.arange(W)[None, :], k[None, None, :])[0]
    od = np.argsort(c.reshape(-1).astype(np.int16), kind="stable"); st = np.searchsorted(c.reshape(-1)[od], np.arange(W + 1))
    for i in range(G - 1):
        if alone and i == 1: continue
        j = 2 if alone and i == 0 else i + 1
        t = C * j + int(o[i]); us = od[st[t]:st[t + 1]] // P; us = us[~np.any(c[us] == C * i + C - 1, axis=1)]
        if len(us):
            x = column(rng, w, us[int(rng.integers(0, len(us)))]); Y[i, C - 1] = x; Y[j, int(o[i])] = x
def setup_inputs_deep(rng):
    X, wt, km, th = base(rng); th = rng.integers(30, 41, th.shape); B = 8 * N; b = np.arange(B)
    X = X.reshape(B, G, C, 16); w = wt.reshape(B, 1, 16).astype(np.int32); k0 = km[:, :, 0].reshape(B, 1, P).astype(np.int32); tries = min(128, max(16, 16 * G // P))
    for i in range(G - 1):
        x = rng.integers(0, 256, (B, tries, 16), dtype=np.int32); u = (np.sum(w * x, axis=2) & (W - 1)).astype(np.int32)
        c = probes(u, k0); o = c & (C - 1); to = np.where((b % 4 == 2) & (i == 0), 2, i + 1)
        hit = ((c >> LC) == to[:, None, None]) & (o != C - 1) & ~np.any(c == C * i + C - 1, axis=2)[..., None]
        like = np.where((b % 4 == 0)[:, None, None], o, np.where((b % 4 == 2)[:, None, None], C - 1 - o, 0)) + 1
        s = np.where(hit, like, 0).reshape(B, -1); a = np.argmax(s, axis=1)
        do = (s[b, a] > 0) & ((b % 2 == 0) | (rng.random(B) < 0.9)) & ((b % 4 != 2) | (i != 1))
        bb = b[do]; aa = a[do]; xs = x[bb, aa // P]
        X[bb, i, C - 1] = xs; X[bb, to[bb], o.reshape(B, -1)[bb, aa]] = xs
    X = X.reshape(N, 8, G, C, 16)
    for g in (3, 4, 7):
        wt[:, g, 0] = 1; wt[:, g, 1] = 16
    for r in range(N): link(rng, X[r, 4], wt[r, 4], km[r, 4, 0], np.full(G, C - 2))
    k = np.arange(2048)
    for g in (3, 7):
        h = int(rng.choice(np.array([3, 5, 7, 9]))); q0 = int(np.argmin((np.arange(C) * h + 1) & (C - 1))); Y = X[:, g].copy()
        for r in range(N):
            u = h - 1 + H * int(rng.integers(0, W // H)); c = (u * u // 32 + k * u) & (W - 1)
            km[r, g, 0] = rng.choice(k[(c & (C - 1)) != C - 1], P); Y[:, r * M:(r + 1) * M, q0] = column(rng, wt[r, g], u)
        for d in range(N): link(rng, Y[d], wt[d, g], km[d, g, 1], np.full(G, C - 2) if g == 3 else 2 * rng.integers(0, C // 2, G), g == 7)
        p = (C * np.arange(G)[:, None] + h * np.arange(C)) & (W - 1)
        for r in range(N):
            kid = np.zeros((G, C, 16), np.int64)
            for d in range(N): kid[(d - r) % N::N] = Y[d, r * M:(r + 1) * M]
            X[r, g, p >> LC, p & (C - 1)] = kid
    return pack(X, wt, km, th)
def setup_inputs_edges(rng):
    X, wt, km, th = base(rng)
    th[:, 0] = 0; e = X[:, 0, :1, C - 1].copy(); X[:, 0, ::2, C - 1] = e; X[:, 0, :, ::4] = e[:, :, None]
    f = rng.integers(0, 16, (N, G, C, 1)); X[:, 1] = (np.arange(16) == f) & (rng.random((N, G, C, 1)) < 0.2); X[:, 1, :, C - 1] = 255; th[:, 1] = 4080
    k = np.arange(2048)
    for q in range(N):
        u = int(255 * np.sum(wt[q, 1])) & (W - 1); c = ((u * u >> 5) + k * u) & (W - 1)
        good = k[(c & (C - 1)) != C - 1]
        km[q, 1, 0] = rng.choice(good if len(good) else k, P)
    km[:, 2] = rng.choice(np.array([0, 1, 3, 2047]), (N, RO, P))
    X[:, 3, ::2, C - 1] = 0; X[:, 3, 0, 0] = 0
    wt[:, 4] = 255; X[:, 4] = 255 - rng.integers(0, 3, (N, G, C, 16))
    X[:, 5, :, C - 1] = rng.integers(0, 256, (N, 1, 16))
    X[:, 6] = 255 * rng.integers(0, 2, (N, G, C, 16)); th[:, 6] = 255 * rng.integers(2, 9, (N, P))
    return pack(X, wt, km, th)
def setup_inputs_far(rng):
    X, wt, km, th = base(rng); k = np.arange(2048)
    for q in range(N):
        for g in (0, 1, 2, 4, 5):
            wt[q, g, 0] |= 1; wt[q, g, 8:] = wt[q, g, :8]
            b = np.concatenate([rng.integers(110, 181, (256, 8)), rng.integers(80, 101, (256, 8))], axis=1); u = np.sum(wt[q, g] * b, axis=1) & (W - 1)
            c = probes(u[None, :], k[None, None, :])[0]
            ok = (c == W - 1) if g == 4 else (c >= 3 * W // 4) & ((c & (C - 1)) != C - 1)
            if g == 5: ok = ok & np.any(c == 0, axis=1)[:, None]
            a, m = np.nonzero(ok); s = int(rng.integers(0, len(a))); x = b[a[s]]; c = c[a[s]]; K = int(m[s]); j = int(c[K]) >> LC; o = int(c[K]) & (C - 1)
            e = rng.integers(35, 71, (G, 8)); e[G // 4:G // 2] = rng.integers(0, 35, (G // 2 - G // 4, 8))
            if g > 2: e[:] = 0
            last = x + np.concatenate([e, -e], axis=1); X[q, g, :, C - 1] = last; km[q, g, 0] = K
            if g == 1:
                km[q, 1, 0] = rng.choice(k[(c & (C - 1)) != C - 1], P); th[q, 1] = rng.integers(2048, 4081, P)
                X[q, 1, :, :C - 1, :8] = rng.integers(0, 41, (G, C - 1, 8)); X[q, 1, :, :C - 1, 8:] = rng.integers(215, 256, (G, C - 1, 8))
            elif g == 4:
                d = rng.integers(1, 60, 16); X[q, 4, G - 1, C - 1] = x - d; th[q, 4] = int(np.sum(d)) + 1
            elif g == 5:
                d = rng.integers(1, 30, 16); X[q, 5, 0, 0] = x - d; X[q, 5, j, o] = x - rng.integers(30, 60, 16)
                km[q, 5, 0, ::2] = int(np.argmax(c == 0)); th[q, 5] = 4080; th[q, 5, ::2] = int(np.sum(d))
            else:
                v = np.repeat(np.array([0, 255]), 8); X[q, g, j, o] = v
                th[q, g] = 4080 if g == 0 else int(np.min(np.sum(np.abs(last - v), axis=1)))
    X[:, 3] = 255 - rng.integers(0, 64, (N, G, C, 16)); X[:, 3, :, C - 1] = rng.integers(0, 64, (N, G, 16)); th[:, 3] = rng.integers(2048, 4081, (N, P))
    return pack(X, wt, km, th)
def setup_inputs_spread(rng):
    X, wt, km, th = base(rng)
    X = np.minimum((rng.random((N, 8, G, C, 16)) * np.exp2(rng.integers(0, 9, (N, 8, G, C, 1)))).astype(np.int64), 255)
    wt = np.clip(np.exp2(8 * rng.random(wt.shape)).astype(np.int64), 1, 255); km = np.clip(np.exp2(11 * rng.random(km.shape)).astype(np.int64) - 1, 0, 2047); km[..., ::2] = rng.integers(0, 2048, km[..., ::2].shape)
    th = rng.integers(0, 4081, th.shape)
    return pack(X, wt, km, th)
def setup_inputs_ties(rng):
    X, wt, km, th = base(rng)
    pat = rng.integers(1, 254, (8, 4, 16)); a = rng.integers(0, 4, (N, 8, G, C))
    X = pat[np.arange(8)[None, :, None, None], a] + rng.integers(0, 2, (N, 8, G, C, 16)); th = rng.integers(3, 11, th.shape)
    return pack(X, wt, km, th)
def check_inputs(d):
    bad = []; v = np.asarray(d["gen0"]).astype(np.float32)
    if not np.all((v >= 0) & (v <= 255) & (v == np.floor(v))): bad.append("gen0 holds other numbers than 0 .. 255")
    for k, lo, hi in (("wt", 1, 255), ("km", 0, 2047), ("th", 0, 4080)):
        if np.min(d[k]) < lo or np.max(d[k]) > hi: bad.append("range of " + k)
    return bad
def reference(gen0, wt, km, th):
    B = 8 * N; X = gen0.astype(np.float32).astype(np.int32).reshape(B, 16, W); w = wt.astype(np.int64).reshape(B, 16, 1)
    kl = np.stack([gentries(a) for a in km]).astype(np.int64).reshape(B, RO, P); tl = np.stack([gentries(a) for a in th]).astype(np.int64).reshape(B, 1, P)
    ar = np.arange(G); q = np.arange(C); rows = np.arange(B)[:, None]
    for t in range(RO):
        x = X[:, :, C - 1::C]
        u = np.sum(w * x, axis=1) & (W - 1)
        c = probes(u, kl[:, t][:, None, :])
        pr = np.take_along_axis(X, c.reshape(B, 1, G * P), 2).reshape(B, 16, G, P)
        D = np.sum(np.abs(pr - x[..., None]), axis=1).astype(np.int64)
        best = np.min(np.where(D < tl, D * W + c, BIG), axis=2)
        j = (best & (W - 1)) >> LC; o = best & (C - 1); ok = (best < BIG) & (j > ar)
        acc = np.full((B, G), BIG, np.int64)
        np.minimum.at(acc, (rows, np.where(ok, j, 0)), np.where(ok, (best - (best & (W - 1))) + ar * C + o, BIG))
        got = acc < BIG; cut = np.where(got, 1 + ((acc & (C - 1)) >> 1), 0); ln = C - cut
        root = np.where(got, (acc & (W - 1)) >> LC, ar)
        for _ in range(LG): root = np.take_along_axis(root, root, 1)
        od = np.argsort(root * G + ar, axis=1)
        ls = np.take_along_axis(ln, od, 1); pos = np.zeros((B, G), np.int64)
        np.put_along_axis(pos, od, np.add.accumulate(ls, axis=1) - ls, 1); L = np.sum(ln, axis=1)
        place = np.where(q < cut[..., None], W, pos[..., None] + q - cut[..., None])
        src = np.zeros((B, W + 1), np.int64); np.put_along_axis(src, place.reshape(B, W), np.arange(W)[None, :], 1)
        p = ((ar * L[:, None]) >> LG)[..., None] + q * (1 + (u & (H - 1)))[..., None]
        p = np.where(p >= L[:, None, None], p - L[:, None, None], p)
        col = np.take_along_axis(src, p.reshape(B, W), 1)
        kid = np.take_along_axis(X, col[:, None, :], 2).reshape(N, 8, 16, G, C); nxt = np.empty_like(kid)
        for r in range(N):
            for d in range(N): nxt[d, :, :, r * M:(r + 1) * M] = kid[r, :, :, (d - r) % N::N]
        X = nxt.reshape(B, 16, W)
    return {"y": np.ascontiguousarray(X.reshape(N, 128, G, C)[..., :YC]).reshape(N, 128, G * YC).astype(np.float32).astype(BF)}

@@ -1,0 +1,430 @@
+import numpy as np
+from concourse.mybir import AluOpType as A, AxisListType, ActivationFunctionType as AF
+
+ROUNDS = 2
+SCRATCH = {}
+DTN = {"b": "bfloat16", "f": "float32", "i": "int32", "u": "uint16"}
+for _w in """X0 4096 b,X1 4096 b,X2 4096 b,XLD 4096 b,XR 4096 b,R8 256x8 b,DF 8192 b,AD 8192 b,wti 1 i,kmi 4 i,thi 2 i,wtf 1 f,kmf 4 f,T4 2 f,
+ipart 1 i,IC 160 f,GM 128 f,IK 256 f,PC 256 f,P16 256 f,CJ 256 f,BNbe 16 f,BNeb 16 f,BN8 8 f,PI 8 i,PF 8 f,PD 16 f,WH 128 b,Zd 144 b,
+ID 128 b,IDn 128 b,Zx0 144 b,Zx1 144 b,BS0 128 b,BS1 128 b,BS2 128 b,jn 8 i,CB 8x8 i,CTb 8x32 b,CTT 8x32 b,CL 8x128 b,CTR 16 f,iT 16 f,W256 16 f,U1 256 i,
+U 256 i,UU 256 i,UB 256 i,CA 512 i,CI 512 i,CU 512 u,HP 256 i,W0 256 f,pen 512 f,km0 256 f,kk 256 f,kt 256 f,M1 128 f,M2 64 f,M3 32 f,best 16 i,Jt 16 i,
+nb 16 f,Jx 16 b,LJ 16 u,PX 272 b,FJ 256 b,NE 16 f,FI 16x32 i,FB 16x32 b,RT 512 b,ACC 16 f,AI 16 i,pt 16 i,zt 16 i,F2 16x16 b,RT2 256 b,R16 256 f,rw 16 f,NTW 16 f,
+SLf 16 f,SL 16 u,RL 16 u,lens 256 f,Lc 1 f,L4 1 f,sk 256 i,sk2 256 i,wp 256 f,pp 256 f,CC 256 u,G 256 f,Yc 256 f,rb 256 b,sti 256 i,
+dd 256 b,TC 256 b,TC2 256 b,Q 256 f,so 256 i,Qm 256 f,bk 16 i,LU 16 u,mo 256 f,ci 256 i,ca 256 i,LL 256 u,PW 13x256 b,YW 13x256 f,YB 4x256 f,LV 4x16 u,
+YT0 512 f,TT0 512 f,OT0 512 f,YT1 512 f,TT1 512 f,OT1 512 f,OB 6x1024 b""".replace("\n", "").split(","):
+    _n, _s, _d = _w.split()
+    SCRATCH[_n] = ("sbuf", [128] + [int(z) for z in _s.split("x")], DTN[_d])
+for _b in range(8):
+    SCRATCH["ps%d" % _b] = ("psum", [128, 512], "float32")
+SEMAPHORES = (["cv", "cs", "ct", "cg", "dwt", "dkm", "dth"] + ["d%s%d" % (x, q) for x in "xy" for q in range(4)]
+              + ["%s%d_%d" % (x, t, k) for x in "al" for t in range(ROUNDS) for k in (1, 2, 3)])
+P24 = 16777216.0
+COPY, ABS = AF.Copy, AF.Abs
+SHR, AND = A.arith_shift_right, A.bitwise_and
+NUM = {n: np.arange(int(np.prod(s[1][1:]))).reshape(s[1][1:]) for n, s in SCRATCH.items()}
+
+
+def rank_program(g, core, T, topo):
+    rank = T.rank_of(core)
+    if rank is None:
+        return
+    v, s, te = g.vector, g.scalar, g.tensor
+
+    def a(n, *ix):
+        ix = tuple((slice(*z) if len(z) else slice(None)) if isinstance(z, tuple) else z for z in ix)
+        ap = T[n][(slice(None),) + ix]
+        if n not in NUM:
+            return ap, []
+        return ap, [(n, NUM[n][ix].reshape(-1) if n[:2] != "ps" else NUM[n])]
+
+    def ind(w, o):
+        return w[0].indirect(o[0]), w[1] + o[1]
+    eng = {"v": v, "s": s, "t": te, "g": g, "y": g.sync}
+    cnt, total, know, snap, ev = {}, {}, {e: {} for e in eng}, {}, []
+    wr = {n: np.full(NUM[n].size, -1) for n in NUM}
+    rd = {n: {} for n in NUM}
+
+    def need(e, reads, writes, cont=False):
+        ids, own = set(), "c" + e
+        for w, lst in ((0, reads), (1, writes)):
+            for n, c in lst:
+                if not (w and cont):
+                    ids.update(np.unique(wr[n][c]).tolist())
+                if w or n[:2] == "ps":
+                    for sm, r in rd[n].items():
+                        if sm != own:
+                            ids.update(np.unique(r[c]).tolist())
+        nd, kn = {}, know[e]
+        for i in ids:
+            if i >= 0:
+                nd[ev[i][0]] = max(nd.get(ev[i][0], 0), ev[i][1])
+        for sm, val in sorted(nd.items(), key=lambda z: z[0] == own):
+            if kn.get(sm, 0) < val:
+                eng[e].wait_ge(T.sem[sm], val)
+                for s2, v2 in list(snap[(sm, val)].items()) + [(sm, val)]:
+                    kn[s2] = max(kn.get(s2, 0), v2)
+
+    def done(e, sm, val, reads, writes):
+        ev.append((sm, val))
+        snap[(sm, val)] = dict(know[e]) if e else {}
+        total[sm] = val
+        for n, c in reads:
+            rd[n].setdefault(sm, np.full(NUM[n].size, -1))[c] = len(ev) - 1
+        for n, c in writes:
+            wr[n][c] = len(ev) - 1
+            for r in rd[n].values():
+                r[c] = -1
+
+    def run(e, call, out, ins, cont=False):
+        reads = [z for x in ins if isinstance(x, tuple) for z in x[1]]
+        need(e, reads, out[1], cont)
+        sm = "c" + e
+        cnt[sm] = cnt.get(sm, 0) + 1
+        call().then_inc(T.sem[sm], 1)
+        done(e, sm, cnt[sm], reads, out[1])
+
+    def dma(e, out, in_, sm):
+        need(e, in_[1], out[1])
+        eng[e].dma_start(out[0], in_[0]).then_inc(T.sem[sm], 16)
+        done(e, sm, 16, in_[1], out[1])
+
+    def z(x):
+        return x[0] if isinstance(x, tuple) else x
+
+    def ts(out, x, s1, o0, s2=None, o1=None):
+        if o1 is None:
+            run("v", lambda: v.tensor_scalar(out[0], x[0], z(s1), None, o0), out, (x, s1))
+        else:
+            run("v", lambda: v.tensor_scalar(out[0], x[0], z(s1), z(s2), o0, o1), out, (x, s1, s2))
+
+    def tt(out, x, y, o):
+        run("v", lambda: v.tensor_tensor(out[0], x[0], y[0], o), out, (x, y))
+
+    def cp(out, x):
+        run("v", lambda: v.tensor_copy(out[0], x[0]), out, (x,))
+
+    def ac(out, x, f=COPY):
+        run("s", lambda: s.activation(out[0], x[0], f), out, (x,))
+
+    def tr(out, x):
+        run("v", lambda: v.transpose(out[0], x[0]), out, (x,))
+
+    def ms(out, c):
+        run("v", lambda: v.memset(out[0], c), out, ())
+
+    def red(out, x, o):
+        run("v", lambda: v.tensor_reduce(out[0], x[0], AxisListType.X, o), out, (x,))
+
+    def scan(out, x, y, o):
+        run("v", lambda: v.tensor_tensor_scan(out[0], x[0], y[0], 0.0, o, o), out, (x, y))
+
+    def iota(out, pat, base=0):
+        run("g", lambda: g.iota(out[0], pat, base, 0, allow_small_or_imprecise_dtypes=True), out, ())
+
+    def mm(out, prs):
+        def call():
+            r = None
+            for n, (l, x) in enumerate(prs):
+                r = te.matmul(out[0], l[0], x[0], n == 0, n == len(prs) - 1)
+            return r
+        run("t", call, out, [x for p in prs for x in p])
+
+    def wrap(ps, *src):
+        for x in range(2):
+            mm(a(ps, (x, 16, 2)), [(a("Zx%d" % x, (16 - 16 * e, 144 - 16 * e)), f(e)) for f in src for e in range(2)])
+
+    def tcol(n):
+        return lambda e: a(n, (16 * e, 256, 32))
+
+    def pf(n):
+        return a("PF", (n, n + 1))
+
+    def pd(n):
+        return a("PD", (n, n + 1))
+
+    halves = [(rank, (rank + 2) % 4), ((rank + 1) % 4, (rank + 3) % 4)]
+    order = halves[0] + halves[1]
+    for q in order:
+        dma("y", a("X0", (1024 * q, 1024 * q + 1024)), a("gen0", (1024 * q, 1024 * q + 1024)), "dx%d" % q)
+    dma("s", a("wti"), a("wt"), "dwt")
+    dma("s", a("kmi"), a("km"), "dkm")
+    dma("s", a("thi"), a("th"), "dth")
+    run("g", lambda: g.iota(T.ipart[:], [[0, 1]], 0, 1), a("ipart"), ())
+    iota(a("GM"), [[16, 8], [0, 16]])
+    iota(a("IC"), [[1, 160]])
+    iota(a("BN8"), [[32, 8]])
+    iota(a("BNbe"), [[32, 8], [0, 2]])
+    iota(a("BNeb"), [[0, 2], [32, 8]])
+    iota(a("FB"), [[0, 512]])
+    iota(a("P16"), [[16, 256]])
+    iota(a("F2"), [[0, 256]])
+    iota(a("PX", (256, 272)), [[0, 16]], 512)
+    iota(a("IK"), [[1, 4], [4, 64]])
+    iota(a("CJ"), [[16, 256]], 15)
+    for t in range(ROUNDS):
+        for n in ("YT", "TT", "OT"):
+            iota(a(n + str(t)), [[0, 512]])
+    ip = a("ipart")
+    for n, m in enumerate((15, 112, 31, 111)):
+        ts(a("PI", (n, n + 1)), ip, m, AND)
+    ts(a("PI", (4, 5)), ip, 4, SHR, 1, AND)
+    ts(a("PI", (5, 6)), ip, 5, SHR)
+    cp(a("PF", (0, 6)), a("PI", (0, 6)))
+    cp(pf(6), ip)
+    ts(pd(0), pf(1), 15.0, A.add)
+    cp(a("wtf"), a("wti"))
+    cp(a("kmf"), a("kmi"))
+    ts(a("T4"), a("thi"), 4096.0, A.mult)
+    ts(a("WH"), a("GM"), pf(1), A.is_equal, a("wtf"), A.mult)
+    ic = a("IC", (0, 144))
+    ts(a("Zd"), ic, pd(0), A.is_equal, 4096.0, A.mult)
+    ts(a("ID"), a("IC", (0, 128)), pf(6), A.is_equal)
+    ts(a("IDn"), a("IC", (0, 128)), pf(6), A.is_equal, -1.0, A.mult)
+
+    def early():
+        for n in range(4):
+            ts(pd(8 + n), pf(5), float(n), A.is_equal)
+        ts(a("jn"), a("BN8"), pf(2), A.add)
+        for f, c in ((16, 4096.0), (17, 1048576.0), (18, 1.0), (19, P24), (20, 16.0)):
+            ms(a("CTb", (), f), c)
+        ms(a("CTb", (), (21, 32)), 0.0)
+        for f in range(8):
+            ts(a("CB", (), f), a("jn"), f, SHR, 1, AND)
+        ts(a("CTb", (), (0, 8)), a("CB"), -P24, A.mult, P24, A.add)
+        ts(a("CTb", (), (8, 16)), a("CB"), P24, A.mult)
+        tr(a("CTT"), a("CTb"))
+        for n in range(4):
+            ts(a("CL", (), (32 * n, 32 * n + 32)), a("CTT"), pd(8 + n), A.mult)
+        ts(a("iT"), a("BNeb"), pf(2), A.add)
+        ts(a("rw"), a("BNbe"), pf(2), A.add)
+        cp(a("FB", (), 20), a("iT"))
+        ts(a("CTR"), a("rw"), 16.0, A.mult, float(4080 * 4096 + 15), A.add)
+        ts(pd(3), pf(0), -1.0, A.mult)
+        ts(pd(4), pf(0), -1.0, A.mult, 4095.0, A.add)
+
+    def late():
+        ts(pd(1), pf(3), 16.0, A.add)
+        ts(pd(2), pf(4), 0.0, A.is_equal)
+        for n in range(3):
+            ts(pd(5 + n), pf(0), float(n), A.is_equal)
+        ts(a("PC"), a("P16"), pf(0), A.add)
+        ts(a("Zx0"), ic, pd(1), A.is_equal, pd(2), A.mult)
+        ts(a("Zx1"), ic, pd(1), A.is_equal, pf(4), A.mult)
+        for n in range(3):
+            ts(a("BS%d" % n), a("GM"), pf(1), A.is_equal, pd(5 + n), A.mult)
+        ts(a("W256"), a("PC", (0, 16)), 256.0, A.add)
+    early()
+    lo, hi, wc = (0, 256), (256, 512), a("ps3", (0, 16))
+
+    for t in range(ROUNDS):
+        xn, nx = "X%d" % t, "X%d" % (t + 1)
+        win = a(xn, (0, 4096))
+
+        def last(q):
+            return a(xn, (1024 * q + 15, 1024 * q + 1024, 16))
+        for hf, ps in zip(halves, ("ps2", "ps3")):
+            for q in hf:
+                i0, i1 = 64 * q, 64 * q + 64
+                mm(a(ps, (i0, i1)), [(a("WH"), last(q))])
+                ac(a("R8", (i0, i1), 0), last(q))
+                ac(a("R8", (i0, i1), 1), last(q))
+                ac(a("R8", (i0, i1), (2, 4)), a("R8", (i0, i1), (0, 2)))
+                ac(a("R8", (i0, i1), (4, 8)), a("R8", (i0, i1), (0, 4)))
+                ac(a("XR", (16 * i0, 16 * i1, 2)), a("R8", (i0, i1), ()))
+
+            def each(f):
+                for q in hf:
+                    f((64 * q, 64 * q + 64))
+
+            def each2(f):
+                for q in hf:
+                    for h in range(2):
+                        f((64 * q, 64 * q + 64), (256 * h + 64 * q, 256 * h + 64 * q + 64), h)
+            each(lambda i: cp(a("U1", i), a(ps, i)))
+            each(lambda i: ts(a("U", i), a("U1", i), 4095, AND))
+            each(lambda i: tt(a("UU", i), a("U", i), a("U", i), A.mult))
+            each2(lambda i, c, h: ts(a("ps6", c), a("U", i), a("kmf", (2 * t + h, 2 * t + h + 1)), A.mult))
+            each(lambda i: ts(a("UB", i), a("UU", i), 5, SHR))
+            each2(lambda i, c, h: tt(a("CA", c), a("ps6", c), a("UB", i), A.add))
+            each2(lambda i, c, h: ts(a("CI", c), a("CA", c), 4095, AND))
+            each2(lambda i, c, h: cp(a("CU", c), a("CI", c)))
+            each(lambda i: cp(a("XR", (16 * i[0] + 1, 16 * i[1], 2)), a("R8", i, ())))
+
+        def chunk(h, g0, n, e):
+            o = 256 * h + g0
+            d, x = (16 * o, 16 * (o + n)), (16 * g0, 16 * (g0 + n))
+            if e == "v":
+                tt(a("DF", d), ind(win, a("CU", (o, o + n))), a("XR", x), A.subtract)
+                ac(a("AD", d), a("DF", d), ABS)
+            else:
+                ac(a("DF", d), ind(win, a("CU", (o, o + n))))
+                for j in range(2):
+                    dj, xj = (d[0] + 512 * j, d[0] + 512 * j + 512), (x[0] + 512 * j, x[0] + 512 * j + 512)
+                    mm(a("ps%d" % (6 + j), (0, 512)), [(a("ID"), a("DF", dj)), (a("IDn"), a("XR", xj))])
+
+            def rest():
+                if e != "v":
+                    for j in range(2):
+                        ac(a("AD", (d[0] + 512 * j, d[0] + 512 * j + 512)), a("ps%d" % (6 + j), (0, 512)), ABS)
+                mm(a("ps%d" % h, (g0, g0 + n)), [(a("Zd", (15 - p, 143 - p)), a("AD", (d[0] + p, d[1], 16))) for p in range(16)])
+            return rest
+        r0 = chunk(1, 64 * order[3], 64, "s")
+        lst = [(0, 64 * q, 64) for q in order] + [(1, 64 * q, 64) for q in order[:2]] + [(1, 64 * order[2] + 32 * j, 32) for j in range(2)]
+        for n, c in enumerate(lst):
+            chunk(*c, "v")()
+            if n == 1:
+                r0()
+        if t == 0:
+            late()
+        for k in range(4):
+            ts(a("HP", (64 * k, 64 * k + 64)), a("U", (k, 256, 4)), 127, AND)
+        ts(a("W0"), a("HP"), pd(3), A.mult, pd(4), A.add)
+        for h, sl in enumerate((lo, hi)):
+            ts(a("pen", sl), a("ps%d" % h, lo), a("T4", (h, h + 1)), A.is_ge, P24, A.mult)
+            tt(a("ps%d" % (5 - h), lo), a("ps%d" % h, lo), a("CI", sl), A.add)
+            tt(a("ps6", lo) if h else a("km0"), a("ps%d" % (5 - h), lo), a("pen", sl), A.max)
+        tt(a("kk"), a("ps6", lo), a("km0"), A.min)
+        tr(a("kt"), a("kk"))
+        tt(a("M1"), a("kt", (0, 256, 2)), a("kt", (1, 256, 2)), A.min)
+        tt(a("M2"), a("M1", (0, 128, 2)), a("M1", (1, 128, 2)), A.min)
+        tt(a("M3"), a("M2", (0, 64, 2)), a("M2", (1, 64, 2)), A.min)
+        for e in range(2):
+            tt(a("best", (8 * e, 8 * e + 8)), a("M3", (2 * e, 32, 4)), a("M3", (2 * e + 1, 32, 4)), A.min)
+        be = a("best")
+        ts(a("Jt"), be, 4, SHR, 255, AND)
+        for f in range(8):
+            ts(a("FI", (), f), be, 4 + f, SHR, 1, AND)
+        ts(a("FI", (), 16), be, 12, SHR, 255, AND)
+        ts(a("FI", (), 17), be, 20, SHR, 31, AND)
+        ts(a("FI", (), 18), be, 1, SHR, 7, AND)
+        tt(a("FI", (), 19), a("Jt"), a("iT"), A.is_le)
+        cp(a("FB", (), (0, 8)), a("FI", (), (0, 8)))
+        ts(a("FB", (), (8, 16)), a("FI", (), (0, 8)), -1.0, A.mult, 1.0, A.add)
+        cp(a("FB", (), (16, 20)), a("FI", (), (16, 20)))
+        tr(a("RT"), a("FB"))
+        for b in range(8):
+            for e in range(2):
+                w = (256 * e, 256 * e + 32 * b + 32)
+                mm(a("ps%d" % b, w), [(a("CL", b, ()), a("RT", w))])
+        ts(a("nb"), a("FI", (), 19), 256.0, A.mult)
+        tt(a("Jx"), a("Jt"), a("nb"), A.max)
+        for b in range(8):
+            for e in range(2):
+                red(a("ACC", (2 * b + e, 2 * b + e + 1)), a("ps%d" % b, (256 * e, 256 * e + 32 * b + 32)), A.min)
+        tt(a("AI"), a("ACC"), a("CTR"), A.min)
+        ts(a("pt"), a("AI"), 4, SHR, 255, AND)
+        ts(a("zt"), a("AI"), 15, AND)
+        cp(a("F2", (), 0), a("pt"))
+        ts(a("F2", (), 1), a("zt"), -1.0, A.mult, 15.0, A.add)
+        ts(a("F2", (), 2), a("zt"), 15.0, A.is_equal, 16.0, A.mult)
+        wrap("ps3", lambda e: a("F2", (e, 16, 2), 0))
+        tr(a("RT2"), a("F2"))
+        mm(a("ps4", lo), [(a("BS0"), a("RT2"))])
+        mm(a("ps5", lo), [(a("BS1"), a("RT2"))])
+        mm(a("ps6", lo), [(a("BS2"), a("RT2"))])
+        wrap("ps0", lambda e: a("Jx", (8 * e, 8 * e + 8)))
+        cp(a("LV", 0, ()), wc)
+        ac(a("PX", lo), a("ps4", lo))
+        cp(a("YW", 0, ()), a("ps5", lo))
+        n = 0
+        YT, TT, OT = ["%s%d" % (x, t) for x in ("YT", "TT", "OT")]
+        for lev in range(4):
+            L = a("LV", lev, ())
+            y0 = a("YB", lev, ())
+            ac(y0, a("YW", n, ()))
+            for _ in range(3):
+                ac(a("PW", n + 1, ()), ind(a("PW", n, ()) if n else a("PX", lo), L))
+                tt(a("YW", n + 1, ()), ind(a("YW", n, ()), L), y0, A.add)
+                n += 1
+            if lev == 0:
+                cp(a("LJ"), a("ps0", (0, 16)))
+                ac(a("FJ"), ind(a("PX", (0, 272)), a("LJ")))
+                ac(a("R16"), a("ps6", lo))
+            tr(a("TC"), a("PW", n, ()))
+            wrap("ps3", tcol("TC"))
+            if lev == 0:
+                tr(a("TC2"), a("FJ"))
+                wrap("ps7", tcol("TC2"))
+            elif lev == 1:
+                tt(a("lens"), a("R16"), a("ps5", lo), A.add)
+                red(a("Lc"), a("lens"), A.add)
+            elif lev == 2:
+                ts(a("sk"), a("IK"), a("Lc"), A.mult)
+                ts(a("L4"), a("Lc"), -1.0, A.mult, 4095.0, A.add)
+                ts(a("sk2"), a("sk"), 8, SHR)
+            else:
+                ts(a("ps6", lo), a("wp"), a("L4"), A.is_le, a("Lc"), A.mult)
+                tt(a("pp"), a("ps6", lo), a("wp"), A.add)
+            if lev < 3:
+                cp(a("LV", lev + 1, ()), wc)
+            if lev == 0:
+                tt(a("NE"), a("ps7", (0, 16)), a("PC", (0, 16)), A.is_equal)
+                tt(a("NTW"), a("NE"), a("W256"), A.mult)
+            elif lev == 2:
+                tt(a("wp"), a("W0"), a("sk2"), A.subtract)
+        yf = a("YW", 12, ())
+        run("s", lambda: s.activation(T.Yc[:], yf[0], AF.Identity, bias=4096.0, scale=-1.0), a("Yc"), (yf,))
+        tt(a("SLf"), wc, a("NTW"), A.max)
+        cp(a("SL"), a("SLf"))
+        cp(a("RL"), wc)
+        cp(ind(a(YT, (0, 512)), a("SL")), yf)
+        scan(a("ps4", lo), a("R16"), a(YT, lo), A.add)
+        tt(a("G"), a(YT, lo), a("ps4", lo), A.subtract)
+        tt(a("rb"), ind(a("G", lo), a("RL")), a("Yc"), A.add)
+        tt(a("sti"), ind(a("G", lo), a("RL")), a("Yc"), A.add)
+        tt(a("dd"), a("sti"), a("rb"), A.subtract)
+        tr(a("TC"), a("rb"))
+        tr(a("TC2"), a("dd"))
+        wrap("ps3", tcol("TC"), tcol("TC2"))
+        ts(a("ps4", lo), a("sti"), 4097.0, A.mult)
+        tt(a("Q"), a("ps4", lo), a("CJ"), A.add)
+        ts(a("so"), a("sti"), 15, AND)
+        ts(a("bk"), wc, 0.125, A.mult, -0.4375, A.add)
+        cp(a("LU"), a("bk"))
+        ts(a("ps5", lo), a("so"), pf(0), A.is_le)
+        tt(a("Qm"), a("ps5", lo), a("Q"), A.mult)
+        cp(ind(a(TT, (0, 512)), a("LU")), a("Q"))
+        ms(a("ps6", (0, 1)), 0.0)
+        cp(ind(a(OT, (0, 512)), a("LU")), a("Qm"))
+        scan(a("ps6", (1, 257)), a(TT, (0, 512, 2)), a(TT, (1, 512, 2)), A.max)
+        tt(a("mo"), a(OT, (0, 512, 2)), a(OT, (1, 512, 2)), A.max)
+        tt(a("ps7", lo), a("ps6", lo), a("mo"), A.max)
+        tt(a("ci"), a("ps7", lo), a("PC"), A.subtract)
+        ts(a("ca"), a("ci"), 4095, AND)
+        cp(a("LL"), a("ca"))
+        cp(a("XLD", (0, 2048)), ind(win, a("LL", (0, 128))))
+        ac(a("XLD", (2048, 4096)), ind(win, a("LL", (128, 256))))
+        cp(a("CC"), a("pp"))
+        mine = (1024 * rank, 1024 * rank + 1024)
+
+        def child(f, k, c0, c1):
+            out = a("OB", 3 * t + k - 1, (c0, c1)) if k else a(nx, (mine[0] + c0, mine[0] + c1))
+            f(out, ind(a("XLD", (0, 4096)), a("CC", (64 * k + c0 // 16, 64 * k + c1 // 16))))
+        for k in (1, 3):
+            child(cp, k, 0, 512)
+            child(ac, k, 512, 1024)
+        child(cp, 2, 0, 1024)
+        child(ac, 0, 0, 1024)
+
+        def engines(src, k):
+            to = T.cores[(T.rank_of(src) + k) % 4]
+            es = topo.engines(src, to)
+            if topo.chip(src) == topo.chip(to):
+                es = [x for x in es if x not in topo.engines(src, T.cores[(T.rank_of(src) + 1) % 4])]
+            return es
+        for k in (1, 3, 2):
+            rid, pid, _ = topo.addr(T.cores[(rank + k) % 4])
+            es = engines(core, k)
+            ob = a("OB", 3 * t + k - 1, ())
+            need("g", ob[1], [])
+            g.remote_dma(a(nx, mine)[0], ob[0], T.sem["a%d_%d" % (t, k)], T.sem["l%d_%d" % (t, k)], pid, rid, sum(1 << x for x in es))
+            total["l%d_%d" % (t, k)] = len(es)
+        for k in (1, 2, 3):
+            fr = (rank - k) % 4
+            done("", "a%d_%d" % (t, k), len(engines(T.cores[fr], k)), [], a(nx, (1024 * fr, 1024 * fr + 1024))[1])
+    for n, q in enumerate(order):
+        c = (1024 * q, 1024 * q + 1024)
+        dma("ys"[n % 2], a("y", c), a("X2", c), "dy%d" % q)
+    for sm in sorted(total):
+        if know["g"].get(sm, 0) < total[sm]:
+            g.wait_ge(T.sem[sm], total[sm])

@@ -5,13 +5,13 @@ ROUNDS = 2
 SCRATCH = {}
 DTN = {"b": "bfloat16", "f": "float32", "i": "int32", "u": "uint16"}
 for _w in """X0 4096 b,X1 4096 b,X2 4096 b,XLD 4096 b,XR 4096 b,R8 256x8 b,DF 8192 b,AD 8192 b,wti 1 i,kmi 4 i,thi 2 i,wtf 1 f,kmf 4 f,T4 2 f,
-ipart 1 i,IC 160 f,GM 128 f,IK 256 f,PC 256 f,P16 256 f,CJ 256 f,BNbe 16 f,BNeb 16 f,BN8 8 f,PI 8 i,PF 8 f,PD 16 f,WH 128 b,Zd 144 b,
-ID 128 b,IDn 128 b,Zx0 144 b,Zx1 144 b,BS0 128 b,BS1 128 b,BS2 128 b,jn 8 i,CB 8x8 i,CTb 8x32 b,CTT 8x32 b,CL 8x128 b,CTR 16 f,iT 16 f,W256 16 f,U1 256 i,
-U 256 i,UU 256 i,UB 256 i,CA 512 i,CI 512 i,CU 512 u,HP 256 i,W0 256 f,pen 512 f,km0 256 f,kk 256 f,kt 256 f,M1 128 f,M2 64 f,M3 32 f,best 16 i,Jt 16 i,
-nb 16 f,Jx 16 b,LJ 16 u,PX 272 b,FJ 256 b,NE 16 f,FI 16x32 i,FB 16x32 b,RT 512 b,ACC 16 f,AI 16 i,pt 16 i,zt 16 i,F2 16x16 b,RT2 256 b,R16 256 f,rw 16 f,NTW 16 f,
-SLf 16 f,SL 16 u,RL 16 u,lens 256 f,Lc 1 f,L4 1 f,sk 256 i,sk2 256 i,wp 256 f,pp 256 f,CC 256 u,G 256 f,Yc 256 f,rb 256 b,sti 256 i,
-dd 256 b,TC 256 b,TC2 256 b,Q 256 f,so 256 i,Qm 256 f,bk 16 i,LU 16 u,mo 256 f,ci 256 i,ca 256 i,LL 256 u,PW 13x256 b,YW 13x256 f,YB 4x256 f,LV 4x16 u,
-YT0 512 f,TT0 512 f,OT0 512 f,YT1 512 f,TT1 512 f,OT1 512 f,OB 6x1024 b""".replace("\n", "").split(","):
+ipart 1 i,IC 160 f,GM 128 f,IK 256 f,IK8 256 f,PC 256 f,P16 256 f,CJ 256 f,BNbe 16 f,BNeb 16 f,PI 8 i,PF 8 f,PD 16 f,WH 128 b,Zd 144 b,
+ID 128 b,IDn 128 b,Zx0 144 b,Zx1 144 b,BS0 128 b,BS1 128 b,BS2 128 b,BSL 128 b,jn 8 i,CB 8x8 i,CTb 8x32 b,CTT 8x32 b,CL 8x128 b,CTR 16 f,iT 16 f,W256 16 f,
+U1 256 i,U 256 i,UU 256 i,UB 256 i,CA 2x256 i,CI 2x256 i,CU 2x256 u,HP 256 i,W0 256 f,pen 512 f,km0 256 f,km1 256 f,kt0 256 f,kt1 256 f,SC0 256 f,SC1 256 f,
+RSi 256 f,RS 256 f,best 16 i,Jt 16 i,nb 16 f,Jx 16 b,LJ 16 u,PX 272 b,FJ 256 b,NE 16 f,FI 16x32 i,FB 16x32 b,RT 512 b,ACC 16 f,AI 16 i,pt 16 i,zt 16 i,
+F2 16x16 b,RT2 256 b,R16 256 f,rw 16 f,NTW 16 f,SLf 16 f,SL 16 u,RL 16 u,Lc 1 f,L4 1 f,sk2 256 i,wp 256 f,pp 256 f,CC 256 u,G 256 f,Yn 256 f,Yc 256 f,
+rb 16 b,sti 256 i,TC 256 b,TC2 256 b,TS 256 i,Q 256 f,so 256 i,Qm 256 f,LU 16 u,ci 256 i,ca 256 i,LL 256 u,PW 13x256 b,YW 13x256 f,YB 4x256 f,LV 4x16 u,
+YT0 528 f,TT0 512 f,OT0 512 f,YT1 528 f,TT1 512 f,OT1 512 f,OB 6x1024 b,bk 16 i""".replace("\n", "").split(","):
     _n, _s, _d = _w.split()
     SCRATCH[_n] = ("sbuf", [128] + [int(z) for z in _s.split("x")], DTN[_d])
 for _b in range(8):
@@ -44,12 +44,11 @@ def rank_program(g, core, T, topo):
     wr = {n: np.full(NUM[n].size, -1) for n in NUM}
     rd = {n: {} for n in NUM}
 
-    def need(e, reads, writes, cont=False):
+    def need(e, reads, writes):
         ids, own = set(), "c" + e
         for w, lst in ((0, reads), (1, writes)):
             for n, c in lst:
-                if not (w and cont):
-                    ids.update(np.unique(wr[n][c]).tolist())
+                ids.update(np.unique(wr[n][c]).tolist())
                 if w or n[:2] == "ps":
                     for sm, r in rd[n].items():
                         if sm != own:
@@ -75,9 +74,9 @@ def rank_program(g, core, T, topo):
             for r in rd[n].values():
                 r[c] = -1
 
-    def run(e, call, out, ins, cont=False):
+    def run(e, call, out, ins):
         reads = [z for x in ins if isinstance(x, tuple) for z in x[1]]
-        need(e, reads, out[1], cont)
+        need(e, reads, out[1])
         sm = "c" + e
         cnt[sm] = cnt.get(sm, 0) + 1
         call().then_inc(T.sem[sm], 1)
@@ -106,6 +105,9 @@ def rank_program(g, core, T, topo):
     def ac(out, x, f=COPY):
         run("s", lambda: s.activation(out[0], x[0], f), out, (x,))
 
+    def lin(out, x, scale, bias, f=AF.Identity):
+        run("s", lambda: s.activation(out[0], x[0], f, bias=z(bias), scale=z(scale)), out, (x, bias, scale))
+
     def tr(out, x):
         run("v", lambda: v.transpose(out[0], x[0]), out, (x,))
 
@@ -115,11 +117,11 @@ def rank_program(g, core, T, topo):
     def red(out, x, o):
         run("v", lambda: v.tensor_reduce(out[0], x[0], AxisListType.X, o), out, (x,))
 
-    def scan(out, x, y, o):
-        run("v", lambda: v.tensor_tensor_scan(out[0], x[0], y[0], 0.0, o, o), out, (x, y))
+    def scan(out, x, y, o0, o1):
+        run("v", lambda: v.tensor_tensor_scan(out[0], x[0], y[0], 0.0, o0, o1), out, (x, y))
 
-    def iota(out, pat, base=0):
-        run("g", lambda: g.iota(out[0], pat, base, 0, allow_small_or_imprecise_dtypes=True), out, ())
+    def iota(out, pat, base=0, cm=0):
+        run("g", lambda: g.iota(out[0], pat, base, cm, allow_small_or_imprecise_dtypes=True), out, ())
 
     def mm(out, prs):
         def call():
@@ -129,9 +131,9 @@ def rank_program(g, core, T, topo):
             return r
         run("t", call, out, [x for p in prs for x in p])
 
-    def wrap(ps, *src):
+    def wrap(ps, f):
         for x in range(2):
-            mm(a(ps, (x, 16, 2)), [(a("Zx%d" % x, (16 - 16 * e, 144 - 16 * e)), f(e)) for f in src for e in range(2)])
+            mm(a(ps, (x, 16, 2)), [(a("Zx%d" % x, (16 - 16 * e, 144 - 16 * e)), f(e)) for e in range(2)])
 
     def tcol(n):
         return lambda e: a(n, (16 * e, 256, 32))
@@ -142,19 +144,24 @@ def rank_program(g, core, T, topo):
     def pd(n):
         return a("PD", (n, n + 1))
 
-    halves = [(rank, (rank + 2) % 4), ((rank + 1) % 4, (rank + 3) % 4)]
-    order = halves[0] + halves[1]
+    order = [(rank + k) % 4 for k in range(4)]
     for q in order:
         dma("y", a("X0", (1024 * q, 1024 * q + 1024)), a("gen0", (1024 * q, 1024 * q + 1024)), "dx%d" % q)
     dma("s", a("wti"), a("wt"), "dwt")
     dma("s", a("kmi"), a("km"), "dkm")
     dma("s", a("thi"), a("th"), "dth")
-    run("g", lambda: g.iota(T.ipart[:], [[0, 1]], 0, 1), a("ipart"), ())
+    iota(a("ipart"), [[0, 1]], 0, 1)
+    iota(a("jn"), [[32, 8]], 0, 1)
     iota(a("GM"), [[16, 8], [0, 16]])
     iota(a("IC"), [[1, 160]])
-    iota(a("BN8"), [[32, 8]])
+    for f, pt in ((5, [[0, 4], [1, 2]]), (6, [[0, 2], [1, 2], [0, 2]]), (7, [[1, 2], [0, 4]])):
+        iota(a("CB", (), f), pt)
+    for f, c in ((8, 4096), (9, 1048576), (10, 1), (20, 16)):
+        iota(a("CTb", (), f), [[0, 8]], c)
+    iota(a("CTb", (), (21, 32)), [[0, 88]])
     iota(a("BNbe"), [[32, 8], [0, 2]])
     iota(a("BNeb"), [[0, 2], [32, 8]])
+    iota(a("RSi"), [[0, 16], [1, 16]])
     iota(a("FB"), [[0, 512]])
     iota(a("P16"), [[16, 256]])
     iota(a("F2"), [[0, 256]])
@@ -162,15 +169,15 @@ def rank_program(g, core, T, topo):
     iota(a("IK"), [[1, 4], [4, 64]])
     iota(a("CJ"), [[16, 256]], 15)
     for t in range(ROUNDS):
-        for n in ("YT", "TT", "OT"):
-            iota(a(n + str(t)), [[0, 512]])
+        for n, w in (("YT", 528), ("TT", 512), ("OT", 512)):
+            iota(a(n + str(t)), [[0, w]])
     ip = a("ipart")
     for n, m in enumerate((15, 112, 31, 111)):
         ts(a("PI", (n, n + 1)), ip, m, AND)
     ts(a("PI", (4, 5)), ip, 4, SHR, 1, AND)
     ts(a("PI", (5, 6)), ip, 5, SHR)
-    cp(a("PF", (0, 6)), a("PI", (0, 6)))
     cp(pf(6), ip)
+    cp(a("PF", (0, 6)), a("PI", (0, 6)))
     ts(pd(0), pf(1), 15.0, A.add)
     cp(a("wtf"), a("wti"))
     cp(a("kmf"), a("kmi"))
@@ -180,133 +187,128 @@ def rank_program(g, core, T, topo):
     ts(a("Zd"), ic, pd(0), A.is_equal, 4096.0, A.mult)
     ts(a("ID"), a("IC", (0, 128)), pf(6), A.is_equal)
     ts(a("IDn"), a("IC", (0, 128)), pf(6), A.is_equal, -1.0, A.mult)
-
-    def early():
-        for n in range(4):
-            ts(pd(8 + n), pf(5), float(n), A.is_equal)
-        ts(a("jn"), a("BN8"), pf(2), A.add)
-        for f, c in ((16, 4096.0), (17, 1048576.0), (18, 1.0), (19, P24), (20, 16.0)):
-            ms(a("CTb", (), f), c)
-        ms(a("CTb", (), (21, 32)), 0.0)
-        for f in range(8):
-            ts(a("CB", (), f), a("jn"), f, SHR, 1, AND)
-        ts(a("CTb", (), (0, 8)), a("CB"), -P24, A.mult, P24, A.add)
-        ts(a("CTb", (), (8, 16)), a("CB"), P24, A.mult)
-        tr(a("CTT"), a("CTb"))
-        for n in range(4):
-            ts(a("CL", (), (32 * n, 32 * n + 32)), a("CTT"), pd(8 + n), A.mult)
-        ts(a("iT"), a("BNeb"), pf(2), A.add)
-        ts(a("rw"), a("BNbe"), pf(2), A.add)
-        cp(a("FB", (), 20), a("iT"))
-        ts(a("CTR"), a("rw"), 16.0, A.mult, float(4080 * 4096 + 15), A.add)
-        ts(pd(3), pf(0), -1.0, A.mult)
-        ts(pd(4), pf(0), -1.0, A.mult, 4095.0, A.add)
+    for f in range(5):
+        ts(a("CB", (), f), a("jn"), f, SHR, 1, AND)
+    for n in range(4):
+        ts(pd(8 + n), pf(5), float(n), A.is_equal)
+    ms(a("CTb", (), 11), P24)
+    ts(a("CTb", (), (0, 8)), a("CB"), -P24, A.mult, P24, A.add)
+    ts(a("CTb", (), (12, 20)), a("CB"), P24, A.mult)
+    tr(a("CTT"), a("CTb"))
 
     def late():
+        lin(pd(3), pf(0), -1.0, 0.0)
+        lin(pd(4), pf(0), -1.0, 4095.0)
+        lin(a("RS"), a("RSi"), -2 * P24, 2 * P24, AF.Relu)
+        lin(a("iT"), a("BNeb"), 1.0, pf(2))
+        ac(a("FB", (), 20), a("iT"))
+        for n in range(4):
+            run("s", lambda: s.activation(T.CL[:, :, 32 * n:32 * n + 32], T.CTT[:], COPY, scale=pd(8 + n)[0]),
+                a("CL", (), (32 * n, 32 * n + 32)), (a("CTT"), pd(8 + n)))
+        lin(a("rw"), a("BNbe"), 1.0, pf(2))
+        lin(a("CTR"), a("rw"), 16.0, float(4080 * 4096 + 15))
+        lin(a("PC"), a("P16"), 1.0, pf(0))
+        lin(a("W256"), a("PC", (0, 16)), 1.0, 256.0)
+        lin(a("IK8"), a("IK"), 1.0 / 256, 0.0)
         ts(pd(1), pf(3), 16.0, A.add)
         ts(pd(2), pf(4), 0.0, A.is_equal)
         for n in range(3):
-            ts(pd(5 + n), pf(0), float(n), A.is_equal)
-        ts(a("PC"), a("P16"), pf(0), A.add)
+            ts(pd(5 + n), pf(0), float(n), A.is_equal, -1.0 if n == 2 else 1.0, A.mult)
         ts(a("Zx0"), ic, pd(1), A.is_equal, pd(2), A.mult)
         ts(a("Zx1"), ic, pd(1), A.is_equal, pf(4), A.mult)
         for n in range(3):
             ts(a("BS%d" % n), a("GM"), pf(1), A.is_equal, pd(5 + n), A.mult)
-        ts(a("W256"), a("PC", (0, 16)), 256.0, A.add)
-    early()
+        tt(a("BSL"), a("BS1"), a("BS2"), A.subtract)
     lo, hi, wc = (0, 256), (256, 512), a("ps3", (0, 16))
+    own, rest = (64 * rank, 64 * rank + 64), [c for c in ((0, 64 * rank), (64 * rank + 64, 256)) if c[0] < c[1]]
 
     for t in range(ROUNDS):
         xn, nx = "X%d" % t, "X%d" % (t + 1)
         win = a(xn, (0, 4096))
 
-        def last(q):
-            return a(xn, (1024 * q + 15, 1024 * q + 1024, 16))
-        for hf, ps in zip(halves, ("ps2", "ps3")):
-            for q in hf:
-                i0, i1 = 64 * q, 64 * q + 64
-                mm(a(ps, (i0, i1)), [(a("WH"), last(q))])
-                ac(a("R8", (i0, i1), 0), last(q))
-                ac(a("R8", (i0, i1), 1), last(q))
-                ac(a("R8", (i0, i1), (2, 4)), a("R8", (i0, i1), (0, 2)))
-                ac(a("R8", (i0, i1), (4, 8)), a("R8", (i0, i1), (0, 4)))
-                ac(a("XR", (16 * i0, 16 * i1, 2)), a("R8", (i0, i1), ()))
+        def last(i):
+            return a(xn, (16 * i[0] + 15, 16 * i[1], 16))
 
-            def each(f):
-                for q in hf:
-                    f((64 * q, 64 * q + 64))
+        def second(i):
+            return (256 + i[0], 256 + i[1])
+        for ps, pcs in (("ps2", [own]), ("ps3", rest)):
+            for i in pcs:
+                mm(a(ps, i), [(a("WH"), last(i))])
+            for f in (lambda i: ac(a("R8", i, 0), last(i)),
+                      lambda i: ac(a("R8", i, 1), last(i)),
+                      lambda i: ac(a("R8", i, (2, 4)), a("R8", i, (0, 2))),
+                      lambda i: ac(a("R8", i, (4, 8)), a("R8", i, (0, 4))),
+                      lambda i: ac(a("XR", (16 * i[0], 16 * i[1], 2)), a("R8", i, ())),
+                      lambda i: cp(a("U1", i), a(ps, i)),
+                      lambda i: ts(a("U", i), a("U1", i), 4095, AND),
+                      lambda i: ts(a("ps6", i), a("U", i), a("kmf", (2 * t, 2 * t + 1)), A.mult),
+                      lambda i: tt(a("UU", i), a("U", i), a("U", i), A.mult),
+                      lambda i: ts(a("ps6", second(i)), a("U", i), a("kmf", (2 * t + 1, 2 * t + 2)), A.mult),
+                      lambda i: ts(a("UB", i), a("UU", i), 5, SHR),
+                      lambda i: tt(a("CA", 0, i), a("ps6", i), a("UB", i), A.add),
+                      lambda i: tt(a("CA", 1, i), a("ps6", second(i)), a("UB", i), A.add),
+                      lambda i: ts(a("CI", (), i), a("CA", (), i), 4095, AND),
+                      lambda i: cp(a("CU", (), i), a("CI", (), i)),
+                      lambda i: cp(a("XR", (16 * i[0] + 1, 16 * i[1], 2)), a("R8", i, ()))):
+                for i in pcs:
+                    f(i)
 
-            def each2(f):
-                for q in hf:
-                    for h in range(2):
-                        f((64 * q, 64 * q + 64), (256 * h + 64 * q, 256 * h + 64 * q + 64), h)
-            each(lambda i: cp(a("U1", i), a(ps, i)))
-            each(lambda i: ts(a("U", i), a("U1", i), 4095, AND))
-            each(lambda i: tt(a("UU", i), a("U", i), a("U", i), A.mult))
-            each2(lambda i, c, h: ts(a("ps6", c), a("U", i), a("kmf", (2 * t + h, 2 * t + h + 1)), A.mult))
-            each(lambda i: ts(a("UB", i), a("UU", i), 5, SHR))
-            each2(lambda i, c, h: tt(a("CA", c), a("ps6", c), a("UB", i), A.add))
-            each2(lambda i, c, h: ts(a("CI", c), a("CA", c), 4095, AND))
-            each2(lambda i, c, h: cp(a("CU", c), a("CI", c)))
-            each(lambda i: cp(a("XR", (16 * i[0] + 1, 16 * i[1], 2)), a("R8", i, ())))
-
-        def chunk(h, g0, n, e):
+        def chunk(h, g0, n, banks=()):
             o = 256 * h + g0
             d, x = (16 * o, 16 * (o + n)), (16 * g0, 16 * (g0 + n))
-            if e == "v":
-                tt(a("DF", d), ind(win, a("CU", (o, o + n))), a("XR", x), A.subtract)
+            if not banks:
+                tt(a("DF", d), ind(win, a("CU", h, (g0, g0 + n))), a("XR", x), A.subtract)
                 ac(a("AD", d), a("DF", d), ABS)
             else:
-                ac(a("DF", d), ind(win, a("CU", (o, o + n))))
-                for j in range(2):
+                ac(a("DF", d), ind(win, a("CU", h, (g0, g0 + n))))
+                for j, b in enumerate(banks):
                     dj, xj = (d[0] + 512 * j, d[0] + 512 * j + 512), (x[0] + 512 * j, x[0] + 512 * j + 512)
-                    mm(a("ps%d" % (6 + j), (0, 512)), [(a("ID"), a("DF", dj)), (a("IDn"), a("XR", xj))])
+                    mm(a(b, (0, 512)), [(a("ID"), a("DF", dj)), (a("IDn"), a("XR", xj))])
 
-            def rest():
-                if e != "v":
-                    for j in range(2):
-                        ac(a("AD", (d[0] + 512 * j, d[0] + 512 * j + 512)), a("ps%d" % (6 + j), (0, 512)), ABS)
+            def end():
+                for j, b in enumerate(banks):
+                    ac(a("AD", (d[0] + 512 * j, d[0] + 512 * j + 512)), a(b, (0, 512)), ABS)
                 mm(a("ps%d" % h, (g0, g0 + n)), [(a("Zd", (15 - p, 143 - p)), a("AD", (d[0] + p, d[1], 16))) for p in range(16)])
-            return rest
-        r0 = chunk(1, 64 * order[3], 64, "s")
-        lst = [(0, 64 * q, 64) for q in order] + [(1, 64 * q, 64) for q in order[:2]] + [(1, 64 * order[2] + 32 * j, 32) for j in range(2)]
-        for n, c in enumerate(lst):
-            chunk(*c, "v")()
-            if n == 1:
+            return end
+        r0 = chunk(1, 64 * order[3], 64, ("ps6", "ps7"))
+        r1 = chunk(1, 64 * order[2] + 32, 32, ("ps4",))
+        for n, c in enumerate([(0, 64 * q, 64) for q in order] + [(1, 64 * q, 64) for q in order[:2]] + [(1, 64 * order[2], 32)]):
+            chunk(*c)()
+            if n == 2:
                 r0()
+            elif n == 4:
+                r1()
         if t == 0:
             late()
         for k in range(4):
             ts(a("HP", (64 * k, 64 * k + 64)), a("U", (k, 256, 4)), 127, AND)
-        ts(a("W0"), a("HP"), pd(3), A.mult, pd(4), A.add)
         for h, sl in enumerate((lo, hi)):
             ts(a("pen", sl), a("ps%d" % h, lo), a("T4", (h, h + 1)), A.is_ge, P24, A.mult)
-            tt(a("ps%d" % (5 - h), lo), a("ps%d" % h, lo), a("CI", sl), A.add)
-            tt(a("ps6", lo) if h else a("km0"), a("ps%d" % (5 - h), lo), a("pen", sl), A.max)
-        tt(a("kk"), a("ps6", lo), a("km0"), A.min)
-        tr(a("kt"), a("kk"))
-        tt(a("M1"), a("kt", (0, 256, 2)), a("kt", (1, 256, 2)), A.min)
-        tt(a("M2"), a("M1", (0, 128, 2)), a("M1", (1, 128, 2)), A.min)
-        tt(a("M3"), a("M2", (0, 64, 2)), a("M2", (1, 64, 2)), A.min)
+            tt(a("ps%d" % (5 - h), lo), a("ps%d" % h, lo), a("CI", h, ()), A.add)
+            if h == 0:
+                ts(a("W0"), a("HP"), pd(3), A.mult, pd(4), A.add)
+            tt(a("km%d" % h), a("ps%d" % (5 - h), lo), a("pen", sl), A.max)
+            tr(a("kt%d" % h), a("km%d" % h))
+            scan(a("SC%d" % h), a("RS"), a("kt%d" % h), A.max, A.min)
         for e in range(2):
-            tt(a("best", (8 * e, 8 * e + 8)), a("M3", (2 * e, 32, 4)), a("M3", (2 * e + 1, 32, 4)), A.min)
+            c = (16 * e + 15, 256, 32)
+            tt(a("best", (8 * e, 8 * e + 8)), a("SC0", c), a("SC1", c), A.min)
         be = a("best")
         ts(a("Jt"), be, 4, SHR, 255, AND)
         for f in range(8):
             ts(a("FI", (), f), be, 4 + f, SHR, 1, AND)
-        ts(a("FI", (), 16), be, 12, SHR, 255, AND)
-        ts(a("FI", (), 17), be, 20, SHR, 31, AND)
-        ts(a("FI", (), 18), be, 1, SHR, 7, AND)
-        tt(a("FI", (), 19), a("Jt"), a("iT"), A.is_le)
-        cp(a("FB", (), (0, 8)), a("FI", (), (0, 8)))
-        ts(a("FB", (), (8, 16)), a("FI", (), (0, 8)), -1.0, A.mult, 1.0, A.add)
-        cp(a("FB", (), (16, 20)), a("FI", (), (16, 20)))
+        ts(a("FI", (), 8), be, 12, SHR, 255, AND)
+        ts(a("FI", (), 9), be, 20, SHR, 31, AND)
+        ts(a("FI", (), 10), be, 1, SHR, 7, AND)
+        tt(a("FI", (), 11), a("Jt"), a("iT"), A.is_le)
+        ts(a("FB", (), (12, 20)), a("FI", (), (0, 8)), -1.0, A.mult, 1.0, A.add)
+        cp(a("FB", (), (0, 12)), a("FI", (), (0, 12)))
         tr(a("RT"), a("FB"))
         for b in range(8):
             for e in range(2):
                 w = (256 * e, 256 * e + 32 * b + 32)
                 mm(a("ps%d" % b, w), [(a("CL", b, ()), a("RT", w))])
-        ts(a("nb"), a("FI", (), 19), 256.0, A.mult)
+        ts(a("nb"), a("FI", (), 11), 256.0, A.mult)
         tt(a("Jx"), a("Jt"), a("nb"), A.max)
         for b in range(8):
             for e in range(2):
@@ -315,23 +317,26 @@ def rank_program(g, core, T, topo):
         ts(a("pt"), a("AI"), 4, SHR, 255, AND)
         ts(a("zt"), a("AI"), 15, AND)
         cp(a("F2", (), 0), a("pt"))
+        ts(a("F2", (), 2), a("AI"), float(4080 * 4096), A.is_ge, 16.0, A.mult)
         ts(a("F2", (), 1), a("zt"), -1.0, A.mult, 15.0, A.add)
-        ts(a("F2", (), 2), a("zt"), 15.0, A.is_equal, 16.0, A.mult)
         wrap("ps3", lambda e: a("F2", (e, 16, 2), 0))
         tr(a("RT2"), a("F2"))
         mm(a("ps4", lo), [(a("BS0"), a("RT2"))])
         mm(a("ps5", lo), [(a("BS1"), a("RT2"))])
+        mm(a("ps7", lo), [(a("BSL"), a("RT2"))])
         mm(a("ps6", lo), [(a("BS2"), a("RT2"))])
         wrap("ps0", lambda e: a("Jx", (8 * e, 8 * e + 8)))
         cp(a("LV", 0, ()), wc)
         ac(a("PX", lo), a("ps4", lo))
         cp(a("YW", 0, ()), a("ps5", lo))
+        cp(a("YB", 0, ()), a("ps5", lo))
         n = 0
         YT, TT, OT = ["%s%d" % (x, t) for x in ("YT", "TT", "OT")]
         for lev in range(4):
             L = a("LV", lev, ())
             y0 = a("YB", lev, ())
-            ac(y0, a("YW", n, ()))
+            if lev:
+                ac(y0, a("YW", n, ()))
             for _ in range(3):
                 ac(a("PW", n + 1, ()), ind(a("PW", n, ()) if n else a("PX", lo), L))
                 tt(a("YW", n + 1, ()), ind(a("YW", n, ()), L), y0, A.add)
@@ -343,57 +348,51 @@ def rank_program(g, core, T, topo):
             tr(a("TC"), a("PW", n, ()))
             wrap("ps3", tcol("TC"))
             if lev == 0:
-                tr(a("TC2"), a("FJ"))
-                wrap("ps7", tcol("TC2"))
+                red(a("Lc"), a("ps7", lo), A.add)
             elif lev == 1:
-                tt(a("lens"), a("R16"), a("ps5", lo), A.add)
-                red(a("Lc"), a("lens"), A.add)
+                lin(a("L4"), a("Lc"), -1.0, 4095.0)
+                tr(a("TC2"), a("FJ"))
+                wrap("ps0", tcol("TC2"))
+                ts(a("sk2"), a("IK8"), a("Lc"), A.mult, 1.0 / 512 - 0.5, A.add)
             elif lev == 2:
-                ts(a("sk"), a("IK"), a("Lc"), A.mult)
-                ts(a("L4"), a("Lc"), -1.0, A.mult, 4095.0, A.add)
-                ts(a("sk2"), a("sk"), 8, SHR)
+                tt(a("NE"), a("ps0", (0, 16)), a("PC", (0, 16)), A.is_equal)
+                tt(a("wp"), a("W0"), a("sk2"), A.subtract)
             else:
                 ts(a("ps6", lo), a("wp"), a("L4"), A.is_le, a("Lc"), A.mult)
+                tt(a("NTW"), a("NE"), a("W256"), A.mult)
                 tt(a("pp"), a("ps6", lo), a("wp"), A.add)
             if lev < 3:
                 cp(a("LV", lev + 1, ()), wc)
-            if lev == 0:
-                tt(a("NE"), a("ps7", (0, 16)), a("PC", (0, 16)), A.is_equal)
-                tt(a("NTW"), a("NE"), a("W256"), A.mult)
-            elif lev == 2:
-                tt(a("wp"), a("W0"), a("sk2"), A.subtract)
         yf = a("YW", 12, ())
-        run("s", lambda: s.activation(T.Yc[:], yf[0], AF.Identity, bias=4096.0, scale=-1.0), a("Yc"), (yf,))
+        lin(a("Yn"), yf, -1.0, 0.0)
         tt(a("SLf"), wc, a("NTW"), A.max)
-        cp(a("SL"), a("SLf"))
         cp(a("RL"), wc)
-        cp(ind(a(YT, (0, 512)), a("SL")), yf)
-        scan(a("ps4", lo), a("R16"), a(YT, lo), A.add)
-        tt(a("G"), a(YT, lo), a("ps4", lo), A.subtract)
-        tt(a("rb"), ind(a("G", lo), a("RL")), a("Yc"), A.add)
+        cp(a("SL"), a("SLf"))
+        cp(ind(a(YT, (8, 520)), a("SL")), a("Yn"))
+        lin(a("Yc"), yf, -1.0, 4096.0)
+        scan(a("G"), a("R16"), a(YT, (7, 263)), A.add, A.add)
         tt(a("sti"), ind(a("G", lo), a("RL")), a("Yc"), A.add)
-        tt(a("dd"), a("sti"), a("rb"), A.subtract)
-        tr(a("TC"), a("rb"))
-        tr(a("TC2"), a("dd"))
-        wrap("ps3", tcol("TC"), tcol("TC2"))
+        tr(a("TS"), a("sti"))
+        ts(a("bk"), a("TS", (0, 256, 16)), 3, SHR)
         ts(a("ps4", lo), a("sti"), 4097.0, A.mult)
-        tt(a("Q"), a("ps4", lo), a("CJ"), A.add)
+        ts(a("rb"), a("bk"), -256.0, A.add)
         ts(a("so"), a("sti"), 15, AND)
-        ts(a("bk"), wc, 0.125, A.mult, -0.4375, A.add)
-        cp(a("LU"), a("bk"))
+        wrap("ps3", lambda e: a("rb", (e, 16, 2)))
+        tt(a("Q"), a("ps4", lo), a("CJ"), A.add)
         ts(a("ps5", lo), a("so"), pf(0), A.is_le)
+        ms(a("ps6", (0, 1)), 0.0)
+        ts(a("LU"), wc, 256.0, A.add)
         tt(a("Qm"), a("ps5", lo), a("Q"), A.mult)
         cp(ind(a(TT, (0, 512)), a("LU")), a("Q"))
-        ms(a("ps6", (0, 1)), 0.0)
         cp(ind(a(OT, (0, 512)), a("LU")), a("Qm"))
-        scan(a("ps6", (1, 257)), a(TT, (0, 512, 2)), a(TT, (1, 512, 2)), A.max)
-        tt(a("mo"), a(OT, (0, 512, 2)), a(OT, (1, 512, 2)), A.max)
-        tt(a("ps7", lo), a("ps6", lo), a("mo"), A.max)
-        tt(a("ci"), a("ps7", lo), a("PC"), A.subtract)
+        scan(a("ps6", (1, 257)), a(TT, (0, 512, 2)), a(TT, (1, 512, 2)), A.max, A.max)
+        tt(a("ps7", lo), a("ps6", lo), a(OT, (0, 512, 2)), A.max)
+        tt(a("ps5", lo), a("ps7", lo), a(OT, (1, 512, 2)), A.max)
+        tt(a("ci"), a("ps5", lo), a("PC"), A.subtract)
         ts(a("ca"), a("ci"), 4095, AND)
         cp(a("LL"), a("ca"))
-        cp(a("XLD", (0, 2048)), ind(win, a("LL", (0, 128))))
-        ac(a("XLD", (2048, 4096)), ind(win, a("LL", (128, 256))))
+        ac(a("XLD", (1952, 4096)), ind(win, a("LL", (122, 256))))
+        cp(a("XLD", (0, 1952)), ind(win, a("LL", (0, 122))))
         cp(a("CC"), a("pp"))
         mine = (1024 * rank, 1024 * rank + 1024)
 
@@ -422,7 +421,7 @@ def rank_program(g, core, T, topo):
         for k in (1, 2, 3):
             fr = (rank - k) % 4
             done("", "a%d_%d" % (t, k), len(engines(T.cores[fr], k)), [], a(nx, (1024 * fr, 1024 * fr + 1024))[1])
-    for n, q in enumerate(order):
+    for n, q in enumerate((rank, (rank + 2) % 4, (rank + 3) % 4, (rank + 1) % 4)):
         c = (1024 * q, 1024 * q + 1024)
         dma("ys"[n % 2], a("y", c), a("X2", c), "dy%d" % q)
     for sm in sorted(total):

import numpy as np
from concourse.mybir import AluOpType as A, AxisListType, ActivationFunctionType as AF

ROUNDS = 2
SCRATCH = {}
DTN = {"b": "bfloat16", "f": "float32", "i": "int32", "u": "uint16"}
for _w in """X0 4096 b,X1 4096 b,X2 4096 b,XLD 4096 b,XR 4096 b,R8 256x8 b,DF 8192 b,AD 8192 b,wti 1 i,kmi 4 i,thi 2 i,wtf 1 f,kmf 4 f,T4 2 f,
ipart 1 i,IC 160 f,GM 128 f,IK 256 f,IK8 256 f,PC 256 f,P16 256 f,CJ 256 f,BNbe 16 f,BNeb 16 f,PI 8 i,PF 8 f,PD 16 f,WH 128 b,Zd 144 b,
ID 128 b,IDn 128 b,Zx0 144 b,Zx1 144 b,BS0 128 b,BS1 128 b,BS2 128 b,BSL 128 b,jn 8 i,CB 8x8 i,CTb 8x32 b,CTT 8x32 b,CL 8x128 b,CTR 16 f,iT 16 f,W256 16 f,
U1 256 i,U 256 i,UU 256 i,UB 256 i,CA 2x256 i,CI 2x256 i,CU 2x256 u,HP 256 i,W0 256 f,pen 512 f,km0 256 f,km1 256 f,kt0 256 f,kt1 256 f,SC0 256 f,SC1 256 f,
RSi 256 f,RS 256 f,best 16 i,Jt 16 i,nb 16 f,Jx 16 b,LJ 16 u,PX 272 b,FJ 256 b,NE 16 f,FI 16x32 i,FB 16x32 b,RT 512 b,ACC 16 f,AI 16 i,pt 16 i,zt 16 i,
F2 16x16 b,RT2 256 b,R16 256 f,rw 16 f,NTW 16 f,SLf 16 f,SL 16 u,RL 16 u,Lc 1 f,L4 1 f,sk2 256 i,wp 256 f,pp 256 f,CC 256 u,G 256 f,Yn 256 f,Yc 256 f,
rb 16 b,sti 256 i,TC 256 b,TC2 256 b,TS 256 i,Q 256 f,so 256 i,Qm 256 f,LU 16 u,ci 256 i,ca 256 i,LL 256 u,PW 13x256 b,YW 13x256 f,YB 4x256 f,LV 4x16 u,
YT0 528 f,TT0 512 f,OT0 512 f,YT1 528 f,TT1 512 f,OT1 512 f,OB 6x1024 b,bk 16 i""".replace("\n", "").split(","):
    _n, _s, _d = _w.split()
    SCRATCH[_n] = ("sbuf", [128] + [int(z) for z in _s.split("x")], DTN[_d])
for _b in range(8):
    SCRATCH["ps%d" % _b] = ("psum", [128, 512], "float32")
SEMAPHORES = (["cv", "cs", "ct", "cg", "dwt", "dkm", "dth"] + ["d%s%d" % (x, q) for x in "xy" for q in range(4)]
              + ["%s%d_%d" % (x, t, k) for x in "al" for t in range(ROUNDS) for k in (1, 2, 3)])
P24 = 16777216.0
COPY, ABS = AF.Copy, AF.Abs
SHR, AND = A.arith_shift_right, A.bitwise_and
NUM = {n: np.arange(int(np.prod(s[1][1:]))).reshape(s[1][1:]) for n, s in SCRATCH.items()}


def rank_program(g, core, T, topo):
    rank = T.rank_of(core)
    if rank is None:
        return
    v, s, te = g.vector, g.scalar, g.tensor

    def a(n, *ix):
        ix = tuple((slice(*z) if len(z) else slice(None)) if isinstance(z, tuple) else z for z in ix)
        ap = T[n][(slice(None),) + ix]
        if n not in NUM:
            return ap, []
        return ap, [(n, NUM[n][ix].reshape(-1) if n[:2] != "ps" else NUM[n])]

    def ind(w, o):
        return w[0].indirect(o[0]), w[1] + o[1]
    eng = {"v": v, "s": s, "t": te, "g": g, "y": g.sync}
    cnt, total, know, snap, ev = {}, {}, {e: {} for e in eng}, {}, []
    wr = {n: np.full(NUM[n].size, -1) for n in NUM}
    rd = {n: {} for n in NUM}

    def need(e, reads, writes):
        ids, own = set(), "c" + e
        for w, lst in ((0, reads), (1, writes)):
            for n, c in lst:
                ids.update(np.unique(wr[n][c]).tolist())
                if w or n[:2] == "ps":
                    for sm, r in rd[n].items():
                        if sm != own:
                            ids.update(np.unique(r[c]).tolist())
        nd, kn = {}, know[e]
        for i in ids:
            if i >= 0:
                nd[ev[i][0]] = max(nd.get(ev[i][0], 0), ev[i][1])
        for sm, val in sorted(nd.items(), key=lambda z: z[0] == own):
            if kn.get(sm, 0) < val:
                eng[e].wait_ge(T.sem[sm], val)
                for s2, v2 in list(snap[(sm, val)].items()) + [(sm, val)]:
                    kn[s2] = max(kn.get(s2, 0), v2)

    def done(e, sm, val, reads, writes):
        ev.append((sm, val))
        snap[(sm, val)] = dict(know[e]) if e else {}
        total[sm] = val
        for n, c in reads:
            rd[n].setdefault(sm, np.full(NUM[n].size, -1))[c] = len(ev) - 1
        for n, c in writes:
            wr[n][c] = len(ev) - 1
            for r in rd[n].values():
                r[c] = -1

    def run(e, call, out, ins):
        reads = [z for x in ins if isinstance(x, tuple) for z in x[1]]
        need(e, reads, out[1])
        sm = "c" + e
        cnt[sm] = cnt.get(sm, 0) + 1
        call().then_inc(T.sem[sm], 1)
        done(e, sm, cnt[sm], reads, out[1])

    def dma(e, out, in_, sm):
        need(e, in_[1], out[1])
        eng[e].dma_start(out[0], in_[0]).then_inc(T.sem[sm], 16)
        done(e, sm, 16, in_[1], out[1])

    def z(x):
        return x[0] if isinstance(x, tuple) else x

    def ts(out, x, s1, o0, s2=None, o1=None):
        if o1 is None:
            run("v", lambda: v.tensor_scalar(out[0], x[0], z(s1), None, o0), out, (x, s1))
        else:
            run("v", lambda: v.tensor_scalar(out[0], x[0], z(s1), z(s2), o0, o1), out, (x, s1, s2))

    def tt(out, x, y, o):
        run("v", lambda: v.tensor_tensor(out[0], x[0], y[0], o), out, (x, y))

    def cp(out, x):
        run("v", lambda: v.tensor_copy(out[0], x[0]), out, (x,))

    def ac(out, x, f=COPY):
        run("s", lambda: s.activation(out[0], x[0], f), out, (x,))

    def lin(out, x, scale, bias, f=AF.Identity):
        run("s", lambda: s.activation(out[0], x[0], f, bias=z(bias), scale=z(scale)), out, (x, bias, scale))

    def tr(out, x):
        run("v", lambda: v.transpose(out[0], x[0]), out, (x,))

    def ms(out, c):
        run("v", lambda: v.memset(out[0], c), out, ())

    def red(out, x, o):
        run("v", lambda: v.tensor_reduce(out[0], x[0], AxisListType.X, o), out, (x,))

    def scan(out, x, y, o0, o1):
        run("v", lambda: v.tensor_tensor_scan(out[0], x[0], y[0], 0.0, o0, o1), out, (x, y))

    def iota(out, pat, base=0, cm=0):
        run("g", lambda: g.iota(out[0], pat, base, cm, allow_small_or_imprecise_dtypes=True), out, ())

    def mm(out, prs):
        def call():
            r = None
            for n, (l, x) in enumerate(prs):
                r = te.matmul(out[0], l[0], x[0], n == 0, n == len(prs) - 1)
            return r
        run("t", call, out, [x for p in prs for x in p])

    def wrap(ps, f):
        for x in range(2):
            mm(a(ps, (x, 16, 2)), [(a("Zx%d" % x, (16 - 16 * e, 144 - 16 * e)), f(e)) for e in range(2)])

    def tcol(n):
        return lambda e: a(n, (16 * e, 256, 32))

    def pf(n):
        return a("PF", (n, n + 1))

    def pd(n):
        return a("PD", (n, n + 1))

    order = [(rank + k) % 4 for k in range(4)]
    for q in order:
        dma("y", a("X0", (1024 * q, 1024 * q + 1024)), a("gen0", (1024 * q, 1024 * q + 1024)), "dx%d" % q)
    dma("s", a("wti"), a("wt"), "dwt")
    dma("s", a("kmi"), a("km"), "dkm")
    dma("s", a("thi"), a("th"), "dth")
    iota(a("ipart"), [[0, 1]], 0, 1)
    iota(a("jn"), [[32, 8]], 0, 1)
    iota(a("GM"), [[16, 8], [0, 16]])
    iota(a("IC"), [[1, 160]])
    for f, pt in ((5, [[0, 4], [1, 2]]), (6, [[0, 2], [1, 2], [0, 2]]), (7, [[1, 2], [0, 4]])):
        iota(a("CB", (), f), pt)
    for f, c in ((8, 4096), (9, 1048576), (10, 1), (20, 16)):
        iota(a("CTb", (), f), [[0, 8]], c)
    iota(a("CTb", (), (21, 32)), [[0, 88]])
    iota(a("BNbe"), [[32, 8], [0, 2]])
    iota(a("BNeb"), [[0, 2], [32, 8]])
    iota(a("RSi"), [[0, 16], [1, 16]])
    iota(a("FB"), [[0, 512]])
    iota(a("P16"), [[16, 256]])
    iota(a("F2"), [[0, 256]])
    iota(a("PX", (256, 272)), [[0, 16]], 512)
    iota(a("IK"), [[1, 4], [4, 64]])
    iota(a("CJ"), [[16, 256]], 15)
    for t in range(ROUNDS):
        for n, w in (("YT", 528), ("TT", 512), ("OT", 512)):
            iota(a(n + str(t)), [[0, w]])
    ip = a("ipart")
    for n, m in enumerate((15, 112, 31, 111)):
        ts(a("PI", (n, n + 1)), ip, m, AND)
    ts(a("PI", (4, 5)), ip, 4, SHR, 1, AND)
    ts(a("PI", (5, 6)), ip, 5, SHR)
    cp(pf(6), ip)
    cp(a("PF", (0, 6)), a("PI", (0, 6)))
    ts(pd(0), pf(1), 15.0, A.add)
    cp(a("wtf"), a("wti"))
    cp(a("kmf"), a("kmi"))
    ts(a("T4"), a("thi"), 4096.0, A.mult)
    ts(a("WH"), a("GM"), pf(1), A.is_equal, a("wtf"), A.mult)
    ic = a("IC", (0, 144))
    ts(a("Zd"), ic, pd(0), A.is_equal, 4096.0, A.mult)
    ts(a("ID"), a("IC", (0, 128)), pf(6), A.is_equal)
    ts(a("IDn"), a("IC", (0, 128)), pf(6), A.is_equal, -1.0, A.mult)
    for f in range(5):
        ts(a("CB", (), f), a("jn"), f, SHR, 1, AND)
    for n in range(4):
        ts(pd(8 + n), pf(5), float(n), A.is_equal)
    ms(a("CTb", (), 11), P24)
    ts(a("CTb", (), (0, 8)), a("CB"), -P24, A.mult, P24, A.add)
    ts(a("CTb", (), (12, 20)), a("CB"), P24, A.mult)
    tr(a("CTT"), a("CTb"))

    def late():
        lin(pd(3), pf(0), -1.0, 0.0)
        lin(pd(4), pf(0), -1.0, 4095.0)
        lin(a("RS"), a("RSi"), -2 * P24, 2 * P24, AF.Relu)
        lin(a("iT"), a("BNeb"), 1.0, pf(2))
        ac(a("FB", (), 20), a("iT"))
        for n in range(4):
            run("s", lambda: s.activation(T.CL[:, :, 32 * n:32 * n + 32], T.CTT[:], COPY, scale=pd(8 + n)[0]),
                a("CL", (), (32 * n, 32 * n + 32)), (a("CTT"), pd(8 + n)))
        lin(a("rw"), a("BNbe"), 1.0, pf(2))
        lin(a("CTR"), a("rw"), 16.0, float(4080 * 4096 + 15))
        lin(a("PC"), a("P16"), 1.0, pf(0))
        lin(a("W256"), a("PC", (0, 16)), 1.0, 256.0)
        lin(a("IK8"), a("IK"), 1.0 / 256, 0.0)
        ts(pd(1), pf(3), 16.0, A.add)
        ts(pd(2), pf(4), 0.0, A.is_equal)
        for n in range(3):
            ts(pd(5 + n), pf(0), float(n), A.is_equal, -1.0 if n == 2 else 1.0, A.mult)
        ts(a("Zx0"), ic, pd(1), A.is_equal, pd(2), A.mult)
        ts(a("Zx1"), ic, pd(1), A.is_equal, pf(4), A.mult)
        for n in range(3):
            ts(a("BS%d" % n), a("GM"), pf(1), A.is_equal, pd(5 + n), A.mult)
        tt(a("BSL"), a("BS1"), a("BS2"), A.subtract)
    lo, hi, wc = (0, 256), (256, 512), a("ps3", (0, 16))
    own, rest = (64 * rank, 64 * rank + 64), [c for c in ((0, 64 * rank), (64 * rank + 64, 256)) if c[0] < c[1]]

    for t in range(ROUNDS):
        xn, nx = "X%d" % t, "X%d" % (t + 1)
        win = a(xn, (0, 4096))

        def last(i):
            return a(xn, (16 * i[0] + 15, 16 * i[1], 16))

        def second(i):
            return (256 + i[0], 256 + i[1])
        for ps, pcs in (("ps2", [own]), ("ps3", rest)):
            for i in pcs:
                mm(a(ps, i), [(a("WH"), last(i))])
            for f in (lambda i: ac(a("R8", i, 0), last(i)),
                      lambda i: ac(a("R8", i, 1), last(i)),
                      lambda i: ac(a("R8", i, (2, 4)), a("R8", i, (0, 2))),
                      lambda i: ac(a("R8", i, (4, 8)), a("R8", i, (0, 4))),
                      lambda i: ac(a("XR", (16 * i[0], 16 * i[1], 2)), a("R8", i, ())),
                      lambda i: cp(a("U1", i), a(ps, i)),
                      lambda i: ts(a("U", i), a("U1", i), 4095, AND),
                      lambda i: ts(a("ps6", i), a("U", i), a("kmf", (2 * t, 2 * t + 1)), A.mult),
                      lambda i: tt(a("UU", i), a("U", i), a("U", i), A.mult),
                      lambda i: ts(a("ps6", second(i)), a("U", i), a("kmf", (2 * t + 1, 2 * t + 2)), A.mult),
                      lambda i: ts(a("UB", i), a("UU", i), 5, SHR),
                      lambda i: tt(a("CA", 0, i), a("ps6", i), a("UB", i), A.add),
                      lambda i: tt(a("CA", 1, i), a("ps6", second(i)), a("UB", i), A.add),
                      lambda i: ts(a("CI", (), i), a("CA", (), i), 4095, AND),
                      lambda i: cp(a("CU", (), i), a("CI", (), i)),
                      lambda i: cp(a("XR", (16 * i[0] + 1, 16 * i[1], 2)), a("R8", i, ()))):
                for i in pcs:
                    f(i)

        def chunk(h, g0, n, banks=()):
            o = 256 * h + g0
            d, x = (16 * o, 16 * (o + n)), (16 * g0, 16 * (g0 + n))
            if not banks:
                tt(a("DF", d), ind(win, a("CU", h, (g0, g0 + n))), a("XR", x), A.subtract)
                ac(a("AD", d), a("DF", d), ABS)
            else:
                ac(a("DF", d), ind(win, a("CU", h, (g0, g0 + n))))
                for j, b in enumerate(banks):
                    dj, xj = (d[0] + 512 * j, d[0] + 512 * j + 512), (x[0] + 512 * j, x[0] + 512 * j + 512)
                    mm(a(b, (0, 512)), [(a("ID"), a("DF", dj)), (a("IDn"), a("XR", xj))])

            def end():
                for j, b in enumerate(banks):
                    ac(a("AD", (d[0] + 512 * j, d[0] + 512 * j + 512)), a(b, (0, 512)), ABS)
                mm(a("ps%d" % h, (g0, g0 + n)), [(a("Zd", (15 - p, 143 - p)), a("AD", (d[0] + p, d[1], 16))) for p in range(16)])
            return end
        r0 = chunk(1, 64 * order[3], 64, ("ps6", "ps7"))
        r1 = chunk(1, 64 * order[2] + 32, 32, ("ps4",))
        for n, c in enumerate([(0, 64 * q, 64) for q in order] + [(1, 64 * q, 64) for q in order[:2]] + [(1, 64 * order[2], 32)]):
            chunk(*c)()
            if n == 2:
                r0()
            elif n == 4:
                r1()
        if t == 0:
            late()
        for k in range(4):
            ts(a("HP", (64 * k, 64 * k + 64)), a("U", (k, 256, 4)), 127, AND)
        for h, sl in enumerate((lo, hi)):
            ts(a("pen", sl), a("ps%d" % h, lo), a("T4", (h, h + 1)), A.is_ge, P24, A.mult)
            tt(a("ps%d" % (5 - h), lo), a("ps%d" % h, lo), a("CI", h, ()), A.add)
            if h == 0:
                ts(a("W0"), a("HP"), pd(3), A.mult, pd(4), A.add)
            tt(a("km%d" % h), a("ps%d" % (5 - h), lo), a("pen", sl), A.max)
            tr(a("kt%d" % h), a("km%d" % h))
            scan(a("SC%d" % h), a("RS"), a("kt%d" % h), A.max, A.min)
        for e in range(2):
            c = (16 * e + 15, 256, 32)
            tt(a("best", (8 * e, 8 * e + 8)), a("SC0", c), a("SC1", c), A.min)
        be = a("best")
        ts(a("Jt"), be, 4, SHR, 255, AND)
        for f in range(8):
            ts(a("FI", (), f), be, 4 + f, SHR, 1, AND)
        ts(a("FI", (), 8), be, 12, SHR, 255, AND)
        ts(a("FI", (), 9), be, 20, SHR, 31, AND)
        ts(a("FI", (), 10), be, 1, SHR, 7, AND)
        tt(a("FI", (), 11), a("Jt"), a("iT"), A.is_le)
        ts(a("FB", (), (12, 20)), a("FI", (), (0, 8)), -1.0, A.mult, 1.0, A.add)
        cp(a("FB", (), (0, 12)), a("FI", (), (0, 12)))
        tr(a("RT"), a("FB"))
        for b in range(8):
            for e in range(2):
                w = (256 * e, 256 * e + 32 * b + 32)
                mm(a("ps%d" % b, w), [(a("CL", b, ()), a("RT", w))])
        ts(a("nb"), a("FI", (), 11), 256.0, A.mult)
        tt(a("Jx"), a("Jt"), a("nb"), A.max)
        for b in range(8):
            for e in range(2):
                red(a("ACC", (2 * b + e, 2 * b + e + 1)), a("ps%d" % b, (256 * e, 256 * e + 32 * b + 32)), A.min)
        tt(a("AI"), a("ACC"), a("CTR"), A.min)
        ts(a("pt"), a("AI"), 4, SHR, 255, AND)
        ts(a("zt"), a("AI"), 15, AND)
        cp(a("F2", (), 0), a("pt"))
        ts(a("F2", (), 2), a("AI"), float(4080 * 4096), A.is_ge, 16.0, A.mult)
        ts(a("F2", (), 1), a("zt"), -1.0, A.mult, 15.0, A.add)
        wrap("ps3", lambda e: a("F2", (e, 16, 2), 0))
        tr(a("RT2"), a("F2"))
        mm(a("ps4", lo), [(a("BS0"), a("RT2"))])
        mm(a("ps5", lo), [(a("BS1"), a("RT2"))])
        mm(a("ps7", lo), [(a("BSL"), a("RT2"))])
        mm(a("ps6", lo), [(a("BS2"), a("RT2"))])
        wrap("ps0", lambda e: a("Jx", (8 * e, 8 * e + 8)))
        cp(a("LV", 0, ()), wc)
        ac(a("PX", lo), a("ps4", lo))
        cp(a("YW", 0, ()), a("ps5", lo))
        cp(a("YB", 0, ()), a("ps5", lo))
        n = 0
        YT, TT, OT = ["%s%d" % (x, t) for x in ("YT", "TT", "OT")]
        for lev in range(4):
            L = a("LV", lev, ())
            y0 = a("YB", lev, ())
            if lev:
                ac(y0, a("YW", n, ()))
            for _ in range(3):
                ac(a("PW", n + 1, ()), ind(a("PW", n, ()) if n else a("PX", lo), L))
                tt(a("YW", n + 1, ()), ind(a("YW", n, ()), L), y0, A.add)
                n += 1
            if lev == 0:
                cp(a("LJ"), a("ps0", (0, 16)))
                ac(a("FJ"), ind(a("PX", (0, 272)), a("LJ")))
                ac(a("R16"), a("ps6", lo))
            tr(a("TC"), a("PW", n, ()))
            wrap("ps3", tcol("TC"))
            if lev == 0:
                red(a("Lc"), a("ps7", lo), A.add)
            elif lev == 1:
                lin(a("L4"), a("Lc"), -1.0, 4095.0)
                tr(a("TC2"), a("FJ"))
                wrap("ps0", tcol("TC2"))
                ts(a("sk2"), a("IK8"), a("Lc"), A.mult, 1.0 / 512 - 0.5, A.add)
            elif lev == 2:
                tt(a("NE"), a("ps0", (0, 16)), a("PC", (0, 16)), A.is_equal)
                tt(a("wp"), a("W0"), a("sk2"), A.subtract)
            else:
                ts(a("ps6", lo), a("wp"), a("L4"), A.is_le, a("Lc"), A.mult)
                tt(a("NTW"), a("NE"), a("W256"), A.mult)
                tt(a("pp"), a("ps6", lo), a("wp"), A.add)
            if lev < 3:
                cp(a("LV", lev + 1, ()), wc)
        yf = a("YW", 12, ())
        lin(a("Yn"), yf, -1.0, 0.0)
        tt(a("SLf"), wc, a("NTW"), A.max)
        cp(a("RL"), wc)
        cp(a("SL"), a("SLf"))
        cp(ind(a(YT, (8, 520)), a("SL")), a("Yn"))
        lin(a("Yc"), yf, -1.0, 4096.0)
        scan(a("G"), a("R16"), a(YT, (7, 263)), A.add, A.add)
        tt(a("sti"), ind(a("G", lo), a("RL")), a("Yc"), A.add)
        tr(a("TS"), a("sti"))
        ts(a("bk"), a("TS", (0, 256, 16)), 3, SHR)
        ts(a("ps4", lo), a("sti"), 4097.0, A.mult)
        ts(a("rb"), a("bk"), -256.0, A.add)
        ts(a("so"), a("sti"), 15, AND)
        wrap("ps3", lambda e: a("rb", (e, 16, 2)))
        tt(a("Q"), a("ps4", lo), a("CJ"), A.add)
        ts(a("ps5", lo), a("so"), pf(0), A.is_le)
        ms(a("ps6", (0, 1)), 0.0)
        ts(a("LU"), wc, 256.0, A.add)
        tt(a("Qm"), a("ps5", lo), a("Q"), A.mult)
        cp(ind(a(TT, (0, 512)), a("LU")), a("Q"))
        cp(ind(a(OT, (0, 512)), a("LU")), a("Qm"))
        scan(a("ps6", (1, 257)), a(TT, (0, 512, 2)), a(TT, (1, 512, 2)), A.max, A.max)
        tt(a("ps7", lo), a("ps6", lo), a(OT, (0, 512, 2)), A.max)
        tt(a("ps5", lo), a("ps7", lo), a(OT, (1, 512, 2)), A.max)
        tt(a("ci"), a("ps5", lo), a("PC"), A.subtract)
        ts(a("ca"), a("ci"), 4095, AND)
        cp(a("LL"), a("ca"))
        ac(a("XLD", (1952, 4096)), ind(win, a("LL", (122, 256))))
        cp(a("XLD", (0, 1952)), ind(win, a("LL", (0, 122))))
        cp(a("CC"), a("pp"))
        mine = (1024 * rank, 1024 * rank + 1024)

        def child(f, k, c0, c1):
            out = a("OB", 3 * t + k - 1, (c0, c1)) if k else a(nx, (mine[0] + c0, mine[0] + c1))
            f(out, ind(a("XLD", (0, 4096)), a("CC", (64 * k + c0 // 16, 64 * k + c1 // 16))))
        for k in (1, 3):
            child(cp, k, 0, 512)
            child(ac, k, 512, 1024)
        child(cp, 2, 0, 1024)
        child(ac, 0, 0, 1024)

        def engines(src, k):
            to = T.cores[(T.rank_of(src) + k) % 4]
            es = topo.engines(src, to)
            if topo.chip(src) == topo.chip(to):
                es = [x for x in es if x not in topo.engines(src, T.cores[(T.rank_of(src) + 1) % 4])]
            return es
        for k in (1, 3, 2):
            rid, pid, _ = topo.addr(T.cores[(rank + k) % 4])
            es = engines(core, k)
            ob = a("OB", 3 * t + k - 1, ())
            need("g", ob[1], [])
            g.remote_dma(a(nx, mine)[0], ob[0], T.sem["a%d_%d" % (t, k)], T.sem["l%d_%d" % (t, k)], pid, rid, sum(1 << x for x in es))
            total["l%d_%d" % (t, k)] = len(es)
        for k in (1, 2, 3):
            fr = (rank - k) % 4
            done("", "a%d_%d" % (t, k), len(engines(T.cores[fr], k)), [], a(nx, (1024 * fr, 1024 * fr + 1024))[1])
    for n, q in enumerate((rank, (rank + 2) % 4, (rank + 3) % 4, (rank + 1) % 4)):
        c = (1024 * q, 1024 * q + 1024)
        dma("ys"[n % 2], a("y", c), a("X2", c), "dy%d" % q)
    for sm in sorted(total):
        if know["g"].get(sm, 0) < total[sm]:
            g.wait_ge(T.sem[sm], total[sm])
